import numpy as np
import ml_dtypes


def mxq(x, axis, fmt="e4m3"):
    dtype, down = {"e4m3": (ml_dtypes.float8_e4m3fn, 7), "e5m2": (ml_dtypes.float8_e5m2, 14)}[fmt]
    v = np.moveaxis(np.asarray(x, np.float32).astype(ml_dtypes.bfloat16).astype(np.float64), axis, -1)
    blocks = v.reshape(v.shape[:-1] + (-1, 32))
    amax = np.abs(blocks).max(-1, keepdims=True)
    byte = np.maximum(np.where(amax > 0, np.frexp(amax)[1] - 1 + 127, 0) - down, 1)
    scale = np.exp2(byte - 127.0)
    codes = (blocks / scale).astype(np.float32).astype(dtype).astype(np.float64)
    return np.moveaxis((codes * scale).reshape(v.shape), -1, axis)


WIDE = False


def mx_kscale(k):
    if not WIDE:
        return np.ones(k)
    levels = np.array([10, -10, 5, -5, 0])
    if k % 512:
        return np.exp2(np.random.permutation(np.resize(levels, k // 32))).repeat(32)
    a = np.empty((k // 512, 16))
    for p in range(k // 512):
        a[p, :8] = np.random.permutation(np.resize(levels, 8))
        for g in range(8):
            far = levels[np.abs(levels - a[p, g]) >= 10]
            a[p, g + 8] = far[np.random.randint(len(far))]
    return np.exp2(a.ravel()).repeat(32)


def f64(x):
    return np.asarray(x).astype(np.float64)


def striped(idx):
    return np.tile(np.asarray(idx).reshape(-1, 16).T, (8, 1)).astype(np.uint16)


def unstriped(offs):
    return offs[:16].T.reshape(-1).astype(np.int64)


E2M1 = np.array([0.0, 0.5, 1.0, 1.5, 2.0, 3.0, 4.0, 6.0, -0.0, -0.5, -1.0, -1.5, -2.0, -3.0, -4.0, -6.0])


def pack_weight(w, fmt):
    k, n = w.shape
    w = f64(np.asarray(w, np.float32).astype(ml_dtypes.bfloat16)).reshape(k // 32, 32, n)
    amax = np.abs(w).max(1)
    if fmt == "e4m3":
        byte = np.frexp(amax)[1] - 1 + 127 - 7
    else:
        mant, ex = np.frexp(amax / 6.0)
        byte = np.where(mant > 0.5, ex, ex - 1) + 127
    byte = np.clip(np.where(amax > 0, byte, 1), 1, 254)
    scaled = (w * np.exp2(127.0 - byte)[:, None, :]).reshape(k, n).astype(np.float32)
    by_word = np.ascontiguousarray(scaled.reshape(k // 512, 128, 4, n).transpose(0, 1, 3, 2))
    if fmt == "e4m3":
        words = by_word.astype(ml_dtypes.float8_e4m3fn).view(np.uint8)
    else:
        c = by_word.astype(ml_dtypes.float4_e2m1fn).view(np.uint8) & 0xF
        words = (c[..., 0::2] | (c[..., 1::2] << 4)).reshape(k // 512, 128, 2 * n)
    return np.ascontiguousarray(words), np.ascontiguousarray(byte.astype(np.uint8).reshape(k // 512, 16, n))


def unpack_weight(words, scales, fmt):
    g, _, n = scales.shape
    words = np.ascontiguousarray(words).reshape(g, 128, n, -1)
    if fmt == "e4m3":
        vals = words.view(ml_dtypes.float8_e4m3fn).astype(np.float64)
    else:
        nib = np.empty((g, 128, n, 4), np.uint8)
        nib[..., 0::2] = words & 0xF
        nib[..., 1::2] = words >> 4
        vals = E2M1[nib]
    vals = vals * np.repeat(np.exp2(scales.astype(np.float64) - 127.0), 8, axis=1)[..., None]
    return vals.transpose(0, 1, 3, 2).reshape(g * 512, n)


def sgn(shape):
    return np.random.uniform(0.5, 2.0, shape) * np.where(np.random.standard_normal(shape) < 0, -1.0, 1.0)


K, T, J, R, O, U, S, E = 512, 1024, 256, 512, 128, 256, 1024, 256


def setup_inputs():
    n = np.random.standard_normal
    idx = np.random.permutation(T)[:J]
    idx2 = np.random.permutation(J)[:O]
    idx3 = np.random.permutation(S)[:U]
    idx4 = np.random.permutation(E)[:O]
    fk = mx_kscale(K)
    fr = mx_kscale(R)
    xtp = pack_weight(n((K, T)) / fk[:, None], "e2m1")
    wp = pack_weight(n((K, R)) * 1 / np.sqrt(K) * fk[:, None], "e4m3")
    vsp = pack_weight(n((R, S)) * 1 / np.sqrt(R) / fr[:, None], "e4m3")
    return {
        "xt_words": xtp[0],
        "xt_scales": xtp[1],
        "w_words": wp[0],
        "w_scales": wp[1],
        "sg": (0.35 * sgn((R, 1))).astype(np.float32),
        "lo": (np.random.uniform(-1.0, 1.0, (R, 1)) + np.log(fr)[:, None]).astype(np.float32),
        "vs_words": vsp[0],
        "vs_scales": vsp[1],
        "su": (np.random.uniform(0.5, 1.6, (U, 1))).astype(np.float32),
        "offs": striped(idx),
        "offs2": striped(idx2),
        "offs3": striped(idx3),
        "offs4": striped(idx4),
    }


def reference(xt_words, xt_scales, w_words, w_scales, sg, lo, vs_words, vs_scales, su, offs, offs2, offs3, offs4):
    idx = unstriped(offs)
    idx2 = unstriped(offs2)
    idx3 = unstriped(offs3)
    idx4 = unstriped(offs4)
    xtu = unpack_weight(xt_words, xt_scales, "e2m1")
    wu = unpack_weight(w_words, w_scales, "e4m3")
    vsu = unpack_weight(vs_words, vs_scales, "e4m3")
    xtidxg = xtu[:, idx]
    a = wu.T @ xtidxg
    hid = np.exp(a[:, idx2] * f64(sg) + f64(lo))
    vsidx3g = vsu[:, idx3]
    hidq = mxq(hid, 0, "e4m3")
    p = vsidx3g.T @ hidq
    y = np.zeros((U, E))
    y[:, idx4] = p * f64(su)
    return y

@@ -1,0 +1,119 @@
+from contextlib import ExitStack
+
+import concourse.mybir as mybir
+
+K, T, J, R, O, U, S, E = 512, 1024, 256, 512, 128, 256, 1024, 256
+FLOPS = 2 * K * R * J + 2 * R * U * O
+
+F32 = mybir.dt.float32
+BF16 = mybir.dt.bfloat16
+I32 = mybir.dt.int32
+U32 = mybir.dt.uint32
+U16 = mybir.dt.uint16
+U8 = mybir.dt.uint8
+FP8X4 = mybir.dt.float8_e4m3fn_x4
+FP4X4 = mybir.dt.float4_e2m1fn_x4
+ACT = mybir.ActivationFunctionType
+
+P = 128
+PACK = 4
+QUADS = 4
+QUAD = 32
+
+
+def tile_list_prototypes_kernel(tc, xt_words, xt_scales, w_words, w_scales, sg, lo, vs_words, vs_scales, su,
+                                   offs, offs2, offs3, offs4, out):
+    nc = tc.nc
+    with ExitStack() as ctx:
+        sb = ctx.enter_context(tc.tile_pool(name="sb", bufs=1))
+        ps = ctx.enter_context(tc.psum_pool(name="ps", bufs=1))
+
+        tok_list = sb.tile([P, J // 16], U16, name="tok_list")
+        slot_list = sb.tile([P, O // 16], U16, name="slot_list")
+        proto_list = sb.tile([P, U // 16], U16, name="proto_list")
+        col_list = sb.tile([P, O // 16], U16, name="col_list")
+
+        xt_w = sb.tile([P, T], U16, name="xt_w", align_bytes=64)
+        xt_s = sb.tile([P, T], U8, name="xt_s", align_bytes=64)
+        w_w = sb.tile([P, R], I32, name="w_w", align_bytes=64)
+        w_s_rows = sb.tile([PACK, QUADS, R // 4], I32, name="w_s_rows", align_bytes=64)
+        w_s = sb.tile([P, R], U8, name="w_s", align_bytes=64)
+        vs_w = sb.tile([P, S], I32, name="vs_w", align_bytes=64)
+        vs_s = sb.tile([P, S], U8, name="vs_s", align_bytes=64)
+        slope = sb.tile([P, PACK], F32, name="slope")
+        level = sb.tile([P, PACK], F32, name="level")
+        weight = sb.tile([P, U // P], F32, name="weight")
+        pages = [sb.tile([P, E], F32, name=f"page{h}") for h in range(U // P)]
+
+        nc.vector.memset(xt_s[:].bitcast(I32), 0)
+        nc.vector.memset(w_s[:].bitcast(I32), 0)
+        nc.vector.memset(vs_s[:].bitcast(I32), 0)
+        for page in pages:
+            nc.vector.memset(page[:], 0.0)
+
+        def load_scale_rows(queue, plane, scales, q):
+            queue.dma_start(out=plane[QUAD * q : QUAD * q + PACK, :].bitcast(I32),
+                            in_=scales[0, PACK * q : PACK * (q + 1), :].bitcast(I32))
+
+        nc.sync.dma_start(tok_list[:], offs)
+        nc.scalar.dma_start(out=w_s_rows[:], in_=w_scales[0].bitcast(I32).rearrange("(q r) c -> r q c", r=PACK))
+        nc.sync.dma_start(out=xt_w[:].bitcast(I32), in_=xt_words[0].bitcast(I32))
+        nc.scalar.dma_start(out=w_w[:], in_=w_words[0].rearrange("p n t -> p (n t)").bitcast(I32))
+        for q in range(QUADS):
+            load_scale_rows(nc.sync if q % 2 == 0 else nc.scalar, xt_s, xt_scales, q)
+        nc.sync.dma_start(out=vs_w[:], in_=vs_words[0].rearrange("p n t -> p (n t)").bitcast(I32))
+        nc.sync.dma_start(slot_list[:], offs2)
+        nc.sync.dma_start(out=slope[:], in_=sg.rearrange("(p t) o -> p (t o)", t=PACK))
+        nc.sync.dma_start(out=level[:], in_=lo.rearrange("(p t) o -> p (t o)", t=PACK))
+        nc.sync.dma_start(proto_list[:], offs3)
+        for q in range(QUADS):
+            load_scale_rows(nc.sync if q < QUADS - 1 else nc.gpsimd, vs_s, vs_scales, q)
+        nc.sync.dma_start(col_list[:], offs4)
+        with nc.allow_non_contiguous_dma(reason="one weight a partition and page"):
+            nc.gpsimd.dma_start(out=weight[:], in_=su.rearrange("(h p) o -> p (h o)", p=P))
+
+        for q in range(QUADS):
+            nc.vector.tensor_copy(out=w_s[QUAD * q : QUAD * q + PACK, :].bitcast(I32), in_=w_s_rows[:, q, :])
+
+        xg_s = sb.tile([P, J], U8, name="xg_s", tag="gathered_s", align_bytes=64)
+        xg_w = sb.tile([P, J], U16, name="xg_w", tag="gathered_w", align_bytes=64)
+        nc.vector.tensor_copy(out=xg_s[:], in_=xt_s[:].indirect(tok_list[:]))
+        nc.vector.tensor_copy(out=xg_w[:], in_=xt_w[:].indirect(tok_list[:]))
+
+        w_by_t = w_w[:].bitcast(U32).rearrange("p (m t) -> p m t", t=PACK)
+        wd_w = [sb.tile([P, 2, P], U32, name=f"wd_w{i}", align_bytes=64) for i in range(2)]
+        for i in range(2):
+            nc.scalar.copy(out=wd_w[i][:].rearrange("p t m -> p m t"), in_=w_by_t[:, :, 2 * i : 2 * i + 2])
+        wd_s = [sb.tile([P, P], U8, name=f"wd_s{t}", align_bytes=64) for t in range(PACK)]
+        for t in range(PACK):
+            nc.vector.tensor_copy(out=wd_s[t][:], in_=w_s[:, t:R:PACK])
+
+        hid = sb.tile([P, PACK * O], BF16, name="hid", align_bytes=64)
+        for t in range(PACK):
+            a_ps = ps.tile([P, J], F32, name=f"a_ps{t}")
+            nc.tensor.matmul_mx(out=a_ps[:], lhsT=wd_w[t // 2][:, t % 2, :].bitcast(FP8X4), lhsT_scale=wd_s[t][:],
+                                rhs=xg_w[:].bitcast(FP4X4), rhs_scale=xg_s[:], start=True, stop=True)
+            a_sb = sb.tile([P, J], F32, name=f"a_sb{t}")
+            nc.vector.tensor_copy(out=a_sb[:], in_=a_ps[:])
+            nc.scalar.activation(out=hid[:, t : PACK * O : PACK], in_=a_sb[:].indirect(slot_list[:]), func=ACT.Exp,
+                                 bias=level[:, t : t + 1], scale=slope[:, t : t + 1])
+
+        vg_s = sb.tile([P, U], U8, name="vg_s", tag="gathered_s", align_bytes=64)
+        vg_w = sb.tile([P, U], U32, name="vg_w", tag="gathered_w", align_bytes=64)
+        nc.vector.tensor_copy(out=vg_w[:], in_=vs_w[:].bitcast(U32).indirect(proto_list[:]))
+        nc.vector.tensor_copy(out=vg_s[:], in_=vs_s[:].indirect(proto_list[:]))
+
+        hq_w = sb.tile([P, O], U32, name="hq_w", align_bytes=64)
+        hq_s = sb.tile([P, O], U8, name="hq_s", align_bytes=64)
+        nc.vector.quantize_mx(out=hq_w[:].bitcast(FP8X4), scales=hq_s[:], in_=hid[:])
+
+        for h in range(U // P):
+            rows = slice(P * h, P * (h + 1))
+            p_ps = ps.tile([P, O], F32, name=f"p_ps{h}")
+            nc.tensor.matmul_mx(out=p_ps[:], lhsT=vg_w[:, rows].bitcast(FP8X4), lhsT_scale=vg_s[:, rows],
+                                rhs=hq_w[:].bitcast(FP8X4), rhs_scale=hq_s[:], start=True, stop=True)
+            p_sb = sb.tile([P, O], F32, name=f"p_sb{h}")
+            nc.vector.tensor_copy(out=p_sb[:], in_=p_ps[:])
+            nc.scalar.activation(out=pages[h][:].indirect(col_list[:]), in_=p_sb[:], func=ACT.Copy,
+                                 scale=weight[:, h : h + 1])
+            nc.sync.dma_start(out=out[rows, :], in_=pages[h][:])

@@ -26,6 +26,7 @@ def tile_list_prototypes_kernel(tc, xt_words, xt_scales, w_words, w_scales, sg, 
     nc = tc.nc
     with ExitStack() as ctx:
         sb = ctx.enter_context(tc.tile_pool(name="sb", bufs=1))
+        late = ctx.enter_context(tc.tile_pool(name="late", bufs=1))
         ps = ctx.enter_context(tc.psum_pool(name="ps", bufs=1))
 
         tok_list = sb.tile([P, J // 16], U16, name="tok_list")
@@ -33,19 +34,18 @@ def tile_list_prototypes_kernel(tc, xt_words, xt_scales, w_words, w_scales, sg, 
         proto_list = sb.tile([P, U // 16], U16, name="proto_list")
         col_list = sb.tile([P, O // 16], U16, name="col_list")
 
-        xt_w = sb.tile([P, T], U16, name="xt_w", align_bytes=64)
+        xt_w = late.tile([P, T], U16, name="xt_w", align_bytes=64, offset=5120)
         xt_s = sb.tile([P, T], U8, name="xt_s", align_bytes=64)
         w_w = sb.tile([P, R], I32, name="w_w", align_bytes=64)
         w_s_rows = sb.tile([PACK, QUADS, R // 4], I32, name="w_s_rows", align_bytes=64)
         w_s = sb.tile([P, R], U8, name="w_s", align_bytes=64)
-        vs_w = sb.tile([P, S], I32, name="vs_w", align_bytes=64)
-        vs_s = sb.tile([P, S], U8, name="vs_s", align_bytes=64)
+        vs_w = late.tile([P, S], I32, name="vs_w", align_bytes=64, offset=1024)
+        vs_s = late.tile([P, S], U8, name="vs_s", align_bytes=64, offset=0)
         slope = sb.tile([P, PACK], F32, name="slope")
         level = sb.tile([P, PACK], F32, name="level")
         weight = sb.tile([P, U // P], F32, name="weight")
         pages = [sb.tile([P, E], F32, name=f"page{h}") for h in range(U // P)]
 
-        nc.vector.memset(xt_s[:].bitcast(I32), 0)
         nc.vector.memset(w_s[:].bitcast(I32), 0)
         nc.vector.memset(vs_s[:].bitcast(I32), 0)
         for page in pages:
@@ -57,20 +57,22 @@ def tile_list_prototypes_kernel(tc, xt_words, xt_scales, w_words, w_scales, sg, 
 
         nc.sync.dma_start(tok_list[:], offs)
         nc.scalar.dma_start(out=w_s_rows[:], in_=w_scales[0].bitcast(I32).rearrange("(q r) c -> r q c", r=PACK))
-        nc.sync.dma_start(out=xt_w[:].bitcast(I32), in_=xt_words[0].bitcast(I32))
-        nc.scalar.dma_start(out=w_w[:], in_=w_words[0].rearrange("p n t -> p (n t)").bitcast(I32))
         for q in range(QUADS):
-            load_scale_rows(nc.sync if q % 2 == 0 else nc.scalar, xt_s, xt_scales, q)
+            queue = nc.sync if q < QUADS - 1 else nc.scalar
+            queue.dma_start(out=xt_s[QUAD * q : QUAD * (q + 1), :].bitcast(I32),
+                            in_=xt_scales[0, PACK * q : PACK * (q + 1), :].bitcast(I32).partition_broadcast(QUAD // PACK))
+        nc.sync.dma_start(out=xt_w[:].bitcast(I32), in_=xt_words[0].bitcast(I32))
+        nc.sync.dma_start(out=w_w[:], in_=w_words[0].rearrange("p n t -> p (n t)").bitcast(I32))
+        nc.sync.dma_start(proto_list[:], offs3)
         nc.sync.dma_start(out=vs_w[:], in_=vs_words[0].rearrange("p n t -> p (n t)").bitcast(I32))
         nc.sync.dma_start(slot_list[:], offs2)
         nc.sync.dma_start(out=slope[:], in_=sg.rearrange("(p t) o -> p (t o)", t=PACK))
         nc.sync.dma_start(out=level[:], in_=lo.rearrange("(p t) o -> p (t o)", t=PACK))
-        nc.sync.dma_start(proto_list[:], offs3)
         for q in range(QUADS):
-            load_scale_rows(nc.sync if q < QUADS - 1 else nc.gpsimd, vs_s, vs_scales, q)
-        nc.sync.dma_start(col_list[:], offs4)
+            load_scale_rows(nc.sync, vs_s, vs_scales, q)
         with nc.allow_non_contiguous_dma(reason="one weight a partition and page"):
-            nc.gpsimd.dma_start(out=weight[:], in_=su.rearrange("(h p) o -> p (h o)", p=P))
+            nc.sync.dma_start(out=weight[:], in_=su.rearrange("(h p) o -> p (h o)", p=P))
+        nc.sync.dma_start(col_list[:], offs4)
 
         for q in range(QUADS):
             nc.vector.tensor_copy(out=w_s[QUAD * q : QUAD * q + PACK, :].bitcast(I32), in_=w_s_rows[:, q, :])
@@ -84,7 +86,7 @@ def tile_list_prototypes_kernel(tc, xt_words, xt_scales, w_words, w_scales, sg, 
         wd_w = [sb.tile([P, 2, P], U32, name=f"wd_w{i}", align_bytes=64) for i in range(2)]
         for i in range(2):
             nc.scalar.copy(out=wd_w[i][:].rearrange("p t m -> p m t"), in_=w_by_t[:, :, 2 * i : 2 * i + 2])
-        wd_s = [sb.tile([P, P], U8, name=f"wd_s{t}", align_bytes=64) for t in range(PACK)]
+        wd_s = [late.tile([P, P], U8, name=f"wd_s{t}", align_bytes=64, offset=5120 + P * t) for t in range(PACK)]
         for t in range(PACK):
             nc.vector.tensor_copy(out=wd_s[t][:], in_=w_s[:, t:R:PACK])
 
@@ -103,8 +105,8 @@ def tile_list_prototypes_kernel(tc, xt_words, xt_scales, w_words, w_scales, sg, 
         nc.vector.tensor_copy(out=vg_w[:], in_=vs_w[:].bitcast(U32).indirect(proto_list[:]))
         nc.vector.tensor_copy(out=vg_s[:], in_=vs_s[:].indirect(proto_list[:]))
 
-        hq_w = sb.tile([P, O], U32, name="hq_w", align_bytes=64)
-        hq_s = sb.tile([P, O], U8, name="hq_s", align_bytes=64)
+        hq_w = late.tile([P, O], U32, name="hq_w", align_bytes=64, offset=1024)
+        hq_s = late.tile([P, O], U8, name="hq_s", align_bytes=64, offset=0)
         nc.vector.quantize_mx(out=hq_w[:].bitcast(FP8X4), scales=hq_s[:], in_=hid[:])
 
         for h in range(U // P):

@@ -34,20 +34,20 @@ def tile_list_prototypes_kernel(tc, xt_words, xt_scales, w_words, w_scales, sg, 
         proto_list = sb.tile([P, U // 16], U16, name="proto_list")
         col_list = sb.tile([P, O // 16], U16, name="col_list")
 
-        xt_w = late.tile([P, T], U16, name="xt_w", align_bytes=64, offset=5120)
+        xt_w = late.tile([P, T], U16, name="xt_w", align_bytes=64, offset=1024)
         xt_s = sb.tile([P, T], U8, name="xt_s", align_bytes=64)
         w_w = sb.tile([P, R], I32, name="w_w", align_bytes=64)
         w_s_rows = sb.tile([PACK, QUADS, R // 4], I32, name="w_s_rows", align_bytes=64)
         w_s = sb.tile([P, R], U8, name="w_s", align_bytes=64)
-        vs_w = late.tile([P, S], I32, name="vs_w", align_bytes=64, offset=1024)
+        vs_w = sb.tile([P, S], I32, name="vs_w", align_bytes=64)
         vs_s = late.tile([P, S], U8, name="vs_s", align_bytes=64, offset=0)
         slope = sb.tile([P, PACK], F32, name="slope")
         level = sb.tile([P, PACK], F32, name="level")
         weight = sb.tile([P, U // P], F32, name="weight")
         pages = [sb.tile([P, E], F32, name=f"page{h}") for h in range(U // P)]
 
-        nc.vector.memset(w_s[:].bitcast(I32), 0)
         nc.vector.memset(vs_s[:].bitcast(I32), 0)
+        nc.vector.memset(w_s[:].bitcast(I32), 0)
         for page in pages:
             nc.vector.memset(page[:], 0.0)
 
@@ -63,11 +63,11 @@ def tile_list_prototypes_kernel(tc, xt_words, xt_scales, w_words, w_scales, sg, 
                             in_=xt_scales[0, PACK * q : PACK * (q + 1), :].bitcast(I32).partition_broadcast(QUAD // PACK))
         nc.sync.dma_start(out=xt_w[:].bitcast(I32), in_=xt_words[0].bitcast(I32))
         nc.sync.dma_start(out=w_w[:], in_=w_words[0].rearrange("p n t -> p (n t)").bitcast(I32))
-        nc.sync.dma_start(proto_list[:], offs3)
-        nc.sync.dma_start(out=vs_w[:], in_=vs_words[0].rearrange("p n t -> p (n t)").bitcast(I32))
         nc.sync.dma_start(slot_list[:], offs2)
         nc.sync.dma_start(out=slope[:], in_=sg.rearrange("(p t) o -> p (t o)", t=PACK))
         nc.sync.dma_start(out=level[:], in_=lo.rearrange("(p t) o -> p (t o)", t=PACK))
+        nc.sync.dma_start(out=vs_w[:], in_=vs_words[0].rearrange("p n t -> p (n t)").bitcast(I32))
+        nc.sync.dma_start(proto_list[:], offs3)
         for q in range(QUADS):
             load_scale_rows(nc.sync, vs_s, vs_scales, q)
         with nc.allow_non_contiguous_dma(reason="one weight a partition and page"):
@@ -86,11 +86,11 @@ def tile_list_prototypes_kernel(tc, xt_words, xt_scales, w_words, w_scales, sg, 
         wd_w = [sb.tile([P, 2, P], U32, name=f"wd_w{i}", align_bytes=64) for i in range(2)]
         for i in range(2):
             nc.scalar.copy(out=wd_w[i][:].rearrange("p t m -> p m t"), in_=w_by_t[:, :, 2 * i : 2 * i + 2])
-        wd_s = [late.tile([P, P], U8, name=f"wd_s{t}", align_bytes=64, offset=5120 + P * t) for t in range(PACK)]
+        wd_s = [late.tile([P, P], U8, name=f"wd_s{t}", align_bytes=64, offset=1024 + P * t) for t in range(PACK)]
         for t in range(PACK):
             nc.vector.tensor_copy(out=wd_s[t][:], in_=w_s[:, t:R:PACK])
 
-        hid = sb.tile([P, PACK * O], BF16, name="hid", align_bytes=64)
+        hid = sb.tile([P, PACK * O], BF16, name="hid", tag="hid", align_bytes=64)
         for t in range(PACK):
             a_ps = ps.tile([P, J], F32, name=f"a_ps{t}")
             nc.tensor.matmul_mx(out=a_ps[:], lhsT=wd_w[t // 2][:, t % 2, :].bitcast(FP8X4), lhsT_scale=wd_s[t][:],
@@ -100,19 +100,24 @@ def tile_list_prototypes_kernel(tc, xt_words, xt_scales, w_words, w_scales, sg, 
             nc.scalar.activation(out=hid[:, t : PACK * O : PACK], in_=a_sb[:].indirect(slot_list[:]), func=ACT.Exp,
                                  bias=level[:, t : t + 1], scale=slope[:, t : t + 1])
 
+        def gather_words(h, tag):
+            words = sb.tile([P, P], U32, name=f"vg_w{h}", tag=tag, align_bytes=64)
+            nc.vector.tensor_copy(out=words[:], in_=vs_w[:].bitcast(U32).indirect(proto_list[:, 8 * h : 8 * h + 8]))
+            return words
+
+        vg_w = [gather_words(0, "gathered_w")]
         vg_s = sb.tile([P, U], U8, name="vg_s", tag="gathered_s", align_bytes=64)
-        vg_w = sb.tile([P, U], U32, name="vg_w", tag="gathered_w", align_bytes=64)
-        nc.vector.tensor_copy(out=vg_w[:], in_=vs_w[:].bitcast(U32).indirect(proto_list[:]))
         nc.vector.tensor_copy(out=vg_s[:], in_=vs_s[:].indirect(proto_list[:]))
 
-        hq_w = late.tile([P, O], U32, name="hq_w", align_bytes=64, offset=1024)
+        hq_w = sb.tile([P, O], U32, name="hq_w", align_bytes=64)
         hq_s = late.tile([P, O], U8, name="hq_s", align_bytes=64, offset=0)
         nc.vector.quantize_mx(out=hq_w[:].bitcast(FP8X4), scales=hq_s[:], in_=hid[:])
+        vg_w.append(gather_words(1, "hid"))
 
         for h in range(U // P):
             rows = slice(P * h, P * (h + 1))
             p_ps = ps.tile([P, O], F32, name=f"p_ps{h}")
-            nc.tensor.matmul_mx(out=p_ps[:], lhsT=vg_w[:, rows].bitcast(FP8X4), lhsT_scale=vg_s[:, rows],
+            nc.tensor.matmul_mx(out=p_ps[:], lhsT=vg_w[h][:].bitcast(FP8X4), lhsT_scale=vg_s[:, rows],
                                 rhs=hq_w[:].bitcast(FP8X4), rhs_scale=hq_s[:], start=True, stop=True)
             p_sb = sb.tile([P, O], F32, name=f"p_sb{h}")
             nc.vector.tensor_copy(out=p_sb[:], in_=p_ps[:])

from contextlib import ExitStack

import concourse.mybir as mybir

K, T, J, R, O, U, S, E = 512, 1024, 256, 512, 128, 256, 1024, 256
FLOPS = 2 * K * R * J + 2 * R * U * O

F32 = mybir.dt.float32
BF16 = mybir.dt.bfloat16
I32 = mybir.dt.int32
U32 = mybir.dt.uint32
U16 = mybir.dt.uint16
U8 = mybir.dt.uint8
FP8X4 = mybir.dt.float8_e4m3fn_x4
FP4X4 = mybir.dt.float4_e2m1fn_x4
ACT = mybir.ActivationFunctionType

P = 128
PACK = 4
QUADS = 4
QUAD = 32


def tile_list_prototypes_kernel(tc, xt_words, xt_scales, w_words, w_scales, sg, lo, vs_words, vs_scales, su,
                                   offs, offs2, offs3, offs4, out):
    nc = tc.nc
    with ExitStack() as ctx:
        sb = ctx.enter_context(tc.tile_pool(name="sb", bufs=1))
        late = ctx.enter_context(tc.tile_pool(name="late", bufs=1))
        ps = ctx.enter_context(tc.psum_pool(name="ps", bufs=1))

        tok_list = sb.tile([P, J // 16], U16, name="tok_list")
        slot_list = sb.tile([P, O // 16], U16, name="slot_list")
        proto_list = sb.tile([P, U // 16], U16, name="proto_list")
        col_list = sb.tile([P, O // 16], U16, name="col_list")

        xt_w = late.tile([P, T], U16, name="xt_w", align_bytes=64, offset=1024)
        xt_s = sb.tile([P, T], U8, name="xt_s", align_bytes=64)
        w_w = sb.tile([P, R], I32, name="w_w", align_bytes=64)
        w_s_rows = sb.tile([PACK, QUADS, R // 4], I32, name="w_s_rows", align_bytes=64)
        w_s = sb.tile([P, R], U8, name="w_s", align_bytes=64)
        vs_w = sb.tile([P, S], I32, name="vs_w", align_bytes=64)
        vs_s = late.tile([P, S], U8, name="vs_s", align_bytes=64, offset=0)
        slope = sb.tile([P, PACK], F32, name="slope")
        level = sb.tile([P, PACK], F32, name="level")
        weight = sb.tile([P, U // P], F32, name="weight")
        pages = [sb.tile([P, E], F32, name=f"page{h}") for h in range(U // P)]

        nc.vector.memset(vs_s[:].bitcast(I32), 0)
        nc.vector.memset(w_s[:].bitcast(I32), 0)
        for page in pages:
            nc.vector.memset(page[:], 0.0)

        def load_scale_rows(queue, plane, scales, q):
            queue.dma_start(out=plane[QUAD * q : QUAD * q + PACK, :].bitcast(I32),
                            in_=scales[0, PACK * q : PACK * (q + 1), :].bitcast(I32))

        nc.sync.dma_start(tok_list[:], offs)
        nc.scalar.dma_start(out=w_s_rows[:], in_=w_scales[0].bitcast(I32).rearrange("(q r) c -> r q c", r=PACK))
        for q in range(QUADS):
            queue = nc.sync if q < QUADS - 1 else nc.scalar
            queue.dma_start(out=xt_s[QUAD * q : QUAD * (q + 1), :].bitcast(I32),
                            in_=xt_scales[0, PACK * q : PACK * (q + 1), :].bitcast(I32).partition_broadcast(QUAD // PACK))
        nc.sync.dma_start(out=xt_w[:].bitcast(I32), in_=xt_words[0].bitcast(I32))
        nc.sync.dma_start(out=w_w[:], in_=w_words[0].rearrange("p n t -> p (n t)").bitcast(I32))
        nc.sync.dma_start(slot_list[:], offs2)
        nc.sync.dma_start(out=slope[:], in_=sg.rearrange("(p t) o -> p (t o)", t=PACK))
        nc.sync.dma_start(out=level[:], in_=lo.rearrange("(p t) o -> p (t o)", t=PACK))
        nc.sync.dma_start(out=vs_w[:], in_=vs_words[0].rearrange("p n t -> p (n t)").bitcast(I32))
        nc.sync.dma_start(proto_list[:], offs3)
        for q in range(QUADS):
            load_scale_rows(nc.sync, vs_s, vs_scales, q)
        with nc.allow_non_contiguous_dma(reason="one weight a partition and page"):
            nc.sync.dma_start(out=weight[:], in_=su.rearrange("(h p) o -> p (h o)", p=P))
        nc.sync.dma_start(col_list[:], offs4)

        for q in range(QUADS):
            nc.vector.tensor_copy(out=w_s[QUAD * q : QUAD * q + PACK, :].bitcast(I32), in_=w_s_rows[:, q, :])

        xg_s = sb.tile([P, J], U8, name="xg_s", tag="gathered_s", align_bytes=64)
        xg_w = sb.tile([P, J], U16, name="xg_w", tag="gathered_w", align_bytes=64)
        nc.vector.tensor_copy(out=xg_s[:], in_=xt_s[:].indirect(tok_list[:]))
        nc.vector.tensor_copy(out=xg_w[:], in_=xt_w[:].indirect(tok_list[:]))

        w_by_t = w_w[:].bitcast(U32).rearrange("p (m t) -> p m t", t=PACK)
        wd_w = [sb.tile([P, 2, P], U32, name=f"wd_w{i}", align_bytes=64) for i in range(2)]
        for i in range(2):
            nc.scalar.copy(out=wd_w[i][:].rearrange("p t m -> p m t"), in_=w_by_t[:, :, 2 * i : 2 * i + 2])
        wd_s = [late.tile([P, P], U8, name=f"wd_s{t}", align_bytes=64, offset=1024 + P * t) for t in range(PACK)]
        for t in range(PACK):
            nc.vector.tensor_copy(out=wd_s[t][:], in_=w_s[:, t:R:PACK])

        hid = sb.tile([P, PACK * O], BF16, name="hid", tag="hid", align_bytes=64)
        for t in range(PACK):
            a_ps = ps.tile([P, J], F32, name=f"a_ps{t}")
            nc.tensor.matmul_mx(out=a_ps[:], lhsT=wd_w[t // 2][:, t % 2, :].bitcast(FP8X4), lhsT_scale=wd_s[t][:],
                                rhs=xg_w[:].bitcast(FP4X4), rhs_scale=xg_s[:], start=True, stop=True)
            a_sb = sb.tile([P, J], F32, name=f"a_sb{t}")
            nc.vector.tensor_copy(out=a_sb[:], in_=a_ps[:])
            nc.scalar.activation(out=hid[:, t : PACK * O : PACK], in_=a_sb[:].indirect(slot_list[:]), func=ACT.Exp,
                                 bias=level[:, t : t + 1], scale=slope[:, t : t + 1])

        def gather_words(h, tag):
            words = sb.tile([P, P], U32, name=f"vg_w{h}", tag=tag, align_bytes=64)
            nc.vector.tensor_copy(out=words[:], in_=vs_w[:].bitcast(U32).indirect(proto_list[:, 8 * h : 8 * h + 8]))
            return words

        vg_w = [gather_words(0, "gathered_w")]
        vg_s = sb.tile([P, U], U8, name="vg_s", tag="gathered_s", align_bytes=64)
        nc.vector.tensor_copy(out=vg_s[:], in_=vs_s[:].indirect(proto_list[:]))

        hq_w = sb.tile([P, O], U32, name="hq_w", align_bytes=64)
        hq_s = late.tile([P, O], U8, name="hq_s", align_bytes=64, offset=0)
        nc.vector.quantize_mx(out=hq_w[:].bitcast(FP8X4), scales=hq_s[:], in_=hid[:])
        vg_w.append(gather_words(1, "hid"))

        for h in range(U // P):
            rows = slice(P * h, P * (h + 1))
            p_ps = ps.tile([P, O], F32, name=f"p_ps{h}")
            nc.tensor.matmul_mx(out=p_ps[:], lhsT=vg_w[h][:].bitcast(FP8X4), lhsT_scale=vg_s[:, rows],
                                rhs=hq_w[:].bitcast(FP8X4), rhs_scale=hq_s[:], start=True, stop=True)
            p_sb = sb.tile([P, O], F32, name=f"p_sb{h}")
            nc.vector.tensor_copy(out=p_sb[:], in_=p_ps[:])
            nc.scalar.activation(out=pages[h][:].indirect(col_list[:]), in_=p_sb[:], func=ACT.Copy,
                                 scale=weight[:, h : h + 1])
            nc.sync.dma_start(out=out[rows, :], in_=pages[h][:])
